import numpy as np
import ml_dtypes


def mxq(x, axis, fmt="e4m3"):
    dtype, down = {"e4m3": (ml_dtypes.float8_e4m3fn, 7), "e5m2": (ml_dtypes.float8_e5m2, 14)}[fmt]
    v = np.moveaxis(np.asarray(x, np.float32).astype(ml_dtypes.bfloat16).astype(np.float64), axis, -1)
    blocks = v.reshape(v.shape[:-1] + (-1, 32))
    amax = np.abs(blocks).max(-1, keepdims=True)
    byte = np.maximum(np.where(amax > 0, np.frexp(amax)[1] - 1 + 127, 0) - down, 1)
    scale = np.exp2(byte - 127.0)
    codes = (blocks / scale).astype(np.float32).astype(dtype).astype(np.float64)
    return np.moveaxis((codes * scale).reshape(v.shape), -1, axis)


WIDE = False


def mx_kscale(k):
    if not WIDE:
        return np.ones(k)
    levels = np.array([24, -24, 12, -12, 0])
    if k % 512:
        return np.exp2(np.random.permutation(np.resize(levels, k // 32))).repeat(32)
    a = np.empty((k // 512, 16))
    for p in range(k // 512):
        a[p, :8] = np.random.permutation(np.resize(levels, 8))
        for g in range(8):
            far = levels[np.abs(levels - a[p, g]) >= 10]
            a[p, g + 8] = far[np.random.randint(len(far))]
    return np.exp2(a.ravel()).repeat(32)


def f64(x):
    return np.asarray(x).astype(np.float64)


def striped8(idx):
    return np.concatenate([v.reshape(-1, 16).T for v in idx]).astype(np.uint16)


def unstriped8(offs):
    return np.stack([offs[16 * g:16 * g + 16].T.reshape(-1) for g in range(8)]).astype(np.int64)


E2M1 = np.array([0.0, 0.5, 1.0, 1.5, 2.0, 3.0, 4.0, 6.0, -0.0, -0.5, -1.0, -1.5, -2.0, -3.0, -4.0, -6.0])


def pack_weight(w, fmt):
    k, n = w.shape
    w = f64(np.asarray(w, np.float32).astype(ml_dtypes.bfloat16)).reshape(k // 32, 32, n)
    amax = np.abs(w).max(1)
    if fmt == "e4m3":
        byte = np.frexp(amax)[1] - 1 + 127 - 7
    else:
        mant, ex = np.frexp(amax / 6.0)
        byte = np.where(mant > 0.5, ex, ex - 1) + 127
    byte = np.clip(np.where(amax > 0, byte, 1), 1, 254)
    scaled = (w * np.exp2(127.0 - byte)[:, None, :]).reshape(k, n).astype(np.float32)
    by_word = np.ascontiguousarray(scaled.reshape(k // 512, 128, 4, n).transpose(0, 1, 3, 2))
    if fmt == "e4m3":
        words = by_word.astype(ml_dtypes.float8_e4m3fn).view(np.uint8)
    else:
        c = by_word.astype(ml_dtypes.float4_e2m1fn).view(np.uint8) & 0xF
        words = (c[..., 0::2] | (c[..., 1::2] << 4)).reshape(k // 512, 128, 2 * n)
    return np.ascontiguousarray(words), np.ascontiguousarray(byte.astype(np.uint8).reshape(k // 512, 16, n))


def unpack_weight(words, scales, fmt):
    g, _, n = scales.shape
    words = np.ascontiguousarray(words).reshape(g, 128, n, -1)
    if fmt == "e4m3":
        vals = words.view(ml_dtypes.float8_e4m3fn).astype(np.float64)
    else:
        nib = np.empty((g, 128, n, 4), np.uint8)
        nib[..., 0::2] = words & 0xF
        nib[..., 1::2] = words >> 4
        vals = E2M1[nib]
    vals = vals * np.repeat(np.exp2(scales.astype(np.float64) - 127.0), 8, axis=1)[..., None]
    return vals.transpose(0, 1, 3, 2).reshape(g * 512, n)


def planes(y):
    n, m = y.shape
    v = y.astype(np.float32).astype(ml_dtypes.bfloat16).astype(np.float64).reshape(n // 32, 32, m)
    top = np.abs(v).max(1)
    byte = np.clip(np.where(top > 0, np.frexp(top)[1] - 1 + 127 - 7, 1), 1, 254)
    codes = (v * np.exp2(127.0 - byte)[:, None, :]).reshape(n, m).astype(np.float32).astype(ml_dtypes.float8_e4m3fn).view(np.uint8)
    words = codes.reshape(n // 512, 128, 4, m).transpose(0, 1, 3, 2)
    return np.ascontiguousarray(words), np.ascontiguousarray(byte.astype(np.uint8).reshape(n // 512, 16, m))


K, L, N, T, J = 512, 512, 512, 2048, 1024


def setup_inputs():
    n = np.random.standard_normal
    s = mx_kscale(K)[:, None]
    s2 = mx_kscale(L)[:, None]
    p_wa = pack_weight(n((K, N)) / np.sqrt(K) / s, "e2m1")
    return {
        "xT": (n((K, T)) * s).astype(np.float32),
        "wgt": np.repeat(np.random.uniform(0.5, 2.0, (8, J)), 16, axis=0).astype(np.float32),
        "zT": (n((L, T)) * s2).astype(np.float32),
        "wgt2": np.repeat(np.random.uniform(0.5, 2.0, (8, J)), 16, axis=0).astype(np.float32),
        "wa_words": p_wa[0],
        "wa_scales": p_wa[1],
        "wb": (n((L, N)) / np.sqrt(L) / s2).astype(np.float32),
        "offs": striped8(np.stack([np.random.permutation(T)[:J] for _ in range(8)])),
        "offs2": striped8(np.stack([np.random.permutation(T)[:J] for _ in range(8)])),
    }


def reference(xT, wgt, zT, wgt2, wa_words, wa_scales, wb, offs, offs2):
    idx = unstriped8(offs)
    idx2 = unstriped8(offs2)
    rows = np.arange(K)
    xg = f64(wgt)[rows // 4 % 128] * f64(xT)[rows[:, None], idx[rows % 512 // 64]]
    xT_ = mxq(xg, 0, "e4m3")
    rows = np.arange(L)
    xg = f64(wgt2)[rows // 4 % 128] * f64(zT)[rows[:, None], idx2[rows % 512 // 64]]
    zT_ = mxq(xg, 0, "e4m3")
    wa_ = unpack_weight(wa_words, wa_scales, "e2m1")
    wb_ = mxq(f64(wb), 0, "e4m3")
    ya = wa_.T @ xT_
    yb = wb_.T @ zT_
    out_0 = np.maximum(ya, yb)
    return (out_0,) + planes(out_0)

@@ -1,0 +1,181 @@
+from contextlib import ExitStack
+
+import concourse.mybir as mybir
+
+K, L, N, T, J = 512, 512, 512, 2048, 1024
+FLOPS = 2 * (K + L) * N * J
+
+F32 = mybir.dt.float32
+BF16 = mybir.dt.bfloat16
+I32 = mybir.dt.int32
+U32 = mybir.dt.uint32
+U16 = mybir.dt.uint16
+U8 = mybir.dt.uint8
+FP8X4 = mybir.dt.float8_e4m3fn_x4
+FP4X4 = mybir.dt.float4_e2m1fn_x4
+MULT = mybir.AluOpType.mult
+MAX = mybir.AluOpType.max
+
+P = 128
+PACK = 4
+GROUP = 16
+X_PIECE = 512
+CHUNK = 256
+CHUNKS = J // CHUNK
+
+
+def interleave(nc, out, planes):
+    nc.scalar.copy(
+        out=out.rearrange("p (c e) i -> p c i e", e=4),
+        in_=planes.rearrange("p i (c e) -> p c i e", e=4),
+    )
+
+
+def quantise(nc, codes, scales, grouped):
+    nc.vector.quantize_mx(out=codes.bitcast(FP8X4), scales=scales, in_=grouped.rearrange("p j i -> p (j i)"))
+
+
+def tile_list_max_noneP_kernel(
+    tc, xT, wgt, zT, wgt2, wa_words, wa_scales, wb, offs, offs2, out_0, out_1, out_2
+):
+    nc = tc.nc
+    with ExitStack() as ctx:
+        sb = ctx.enter_context(tc.tile_pool(name="sb", bufs=1))
+        psum = ctx.enter_context(tc.psum_pool(name="psum", bufs=4))
+
+        def tile(name, shape, dtype):
+            return sb.tile(shape, dtype, name=name, align_bytes=64)
+
+        x_list = sb.tile([P, J // GROUP], U16, name="x_list")
+        z_list = sb.tile([P, J // GROUP], U16, name="z_list")
+        x_planes = [tile(f"x_plane{i}", [P, T], F32) for i in range(PACK)]
+        z_planes = [tile(f"z_plane{i}", [P, T], F32) for i in range(PACK)]
+        x_wgt = [tile(f"x_wgt{h}", [P, X_PIECE], F32) for h in range(J // X_PIECE)]
+        z_wgt = tile("z_wgt", [P, J], F32)
+        wa_raw = tile("wa_raw", [P, 2 * N], U8)
+        wa_scales_raw = tile("wa_scales_raw", [P, N], U8)
+        wb_raw = tile("wb_raw", [P, PACK, N], F32)
+
+        x_rows = xT.rearrange("(p i) t -> p i t", i=PACK)
+        z_rows = zT.rearrange("(p i) t -> p i t", i=PACK)
+
+        nc.vector.memset(wa_scales_raw[:].bitcast(I32), 0)
+        nc.sync.dma_start(x_list[:], offs)
+        nc.sync.dma_start(x_planes[0][:], x_rows[:, 0, :])
+        nc.scalar.dma_start(wa_raw[:].bitcast(I32), wa_words[0].bitcast(I32))
+        for q in range(4):
+            nc.scalar.dma_start(
+                wa_scales_raw[32 * q : 32 * q + 4, :].bitcast(I32), wa_scales[0, 4 * q : 4 * q + 4, :].bitcast(I32)
+            )
+        for h in range(J // X_PIECE):
+            nc.sync.dma_start(x_wgt[h][:], wgt[:, h * X_PIECE : (h + 1) * X_PIECE])
+        for i in range(1, PACK):
+            nc.sync.dma_start(x_planes[i][:], x_rows[:, i, :])
+        nc.sync.dma_start(wb_raw[:], wb.rearrange("(p i) n -> p i n", i=PACK))
+        nc.sync.dma_start(z_list[:], offs2)
+        nc.sync.dma_start(z_wgt[:], wgt2)
+        for i in range(PACK):
+            nc.sync.dma_start(z_planes[i][:], z_rows[:, i, :])
+
+        wa_codes = tile("wa_codes", [P, 2 * N], U8)
+        wa_plane = tile("wa_plane", [P, N], U8)
+        nc.vector.tensor_copy(
+            out=wa_codes[:].rearrange("p (t m b) -> p m t b", t=PACK, b=2),
+            in_=wa_raw[:].rearrange("p (m t b) -> p m t b", t=PACK, b=2),
+        )
+        nc.vector.tensor_copy(
+            out=wa_plane[:].rearrange("p (t m) -> p m t", t=PACK),
+            in_=wa_scales_raw[:].rearrange("p (m t) -> p m t", t=PACK),
+        )
+
+        def gather(picked, planes, i, offsets, j0, width, weights):
+            nc.vector.tensor_tensor(
+                picked[:, i, :], planes[i][:].indirect(offsets[:, j0 // GROUP : (j0 + width) // GROUP]), weights, MULT
+            )
+
+        def products(lhs_of, codes, scales):
+            banks = []
+            for u in range(2):
+                bank = psum.tile([P, 2, CHUNK], F32, name="bank", bufs=8)
+                for v in range(2):
+                    lhs, lhs_scale = lhs_of(2 * u + v)
+                    nc.tensor.matmul_mx(
+                        out=bank[:, v, :], lhsT=lhs, lhsT_scale=lhs_scale,
+                        rhs=codes.bitcast(FP8X4), rhs_scale=scales, start=True, stop=True,
+                    )
+                banks.append(bank)
+            return banks
+
+        def wa_of(t):
+            return wa_codes[:, 2 * P * t : 2 * P * (t + 1)].bitcast(FP4X4), wa_plane[:, P * t : P * (t + 1)]
+
+        x_picked = [tile(f"x_picked{h}", [P, PACK, X_PIECE], F32) for h in range(J // X_PIECE)]
+        for i in range(PACK):
+            for h in range(J // X_PIECE):
+                gather(x_picked[h], x_planes, i, x_list, h * X_PIECE, X_PIECE, x_wgt[h][:])
+        ya = [tile(f"ya{c}", [P, PACK, CHUNK], F32) for c in range(CHUNKS)]
+        x_grouped = [tile(f"x_grouped{h}", [P, X_PIECE, PACK], BF16) for h in range(J // X_PIECE)]
+        for h in range(J // X_PIECE):
+            interleave(nc, x_grouped[h][:], x_picked[h][:])
+        wb_grouped = tile("wb_grouped", [P, N, PACK], BF16)
+        nc.scalar.copy(
+            out=wb_grouped[:].rearrange("p (t m) i -> p m i t", t=PACK),
+            in_=wb_raw[:].rearrange("p i (m t) -> p m i t", t=PACK),
+        )
+        for h in range(J // X_PIECE):
+            x_codes = tile(f"x_codes{h}", [P, X_PIECE], U32)
+            x_scales = tile(f"x_scales{h}", [P, X_PIECE], U8)
+            quantise(nc, x_codes[:], x_scales[:], x_grouped[h][:])
+            for s in range(X_PIECE // CHUNK):
+                cols = slice(s * CHUNK, (s + 1) * CHUNK)
+                c = h * (X_PIECE // CHUNK) + s
+                for u, bank in enumerate(products(wa_of, x_codes[:, cols], x_scales[:, cols])):
+                    nc.scalar.copy(out=ya[c][:, 2 * u : 2 * u + 2, :], in_=bank[:])
+
+        wb_codes = tile("wb_codes", [P, N], U32)
+        wb_plane = tile("wb_plane", [P, N], U8)
+        quantise(nc, wb_codes[:], wb_plane[:], wb_grouped[:])
+
+        def wb_of(t):
+            return wb_codes[:, P * t : P * (t + 1)].bitcast(FP8X4), wb_plane[:, P * t : P * (t + 1)]
+
+        z_picked = [tile(f"z_picked{c}", [P, PACK, CHUNK], F32) for c in range(CHUNKS)]
+        for i in range(PACK):
+            for c in range(CHUNKS):
+                gather(z_picked[c], z_planes, i, z_list, c * CHUNK, CHUNK, z_wgt[:, c * CHUNK : (c + 1) * CHUNK])
+        z_grouped = [tile(f"z_grouped{c}", [P, CHUNK, PACK], BF16) for c in range(CHUNKS)]
+        for c in range(CHUNKS):
+            interleave(nc, z_grouped[c][:], z_picked[c][:])
+
+        y_codes = tile("y_codes", [P, J], U32)
+        y_scales = tile("y_scales", [P, J], U8)
+        out_rows = out_0.rearrange("(p t) j -> p t j", t=PACK)
+        out_words = out_1[0].rearrange("p j i -> p (j i)").bitcast(I32)
+        y = [tile(f"y{c}", [P, PACK, CHUNK], F32) for c in range(CHUNKS)]
+        y_grouped = [tile(f"y_grouped{c}", [P, CHUNK, PACK], BF16) for c in range(CHUNKS)]
+        yb_banks = []
+        for step in range(CHUNKS + 2):
+            c = step
+            if c < CHUNKS:
+                z_codes = tile(f"z_codes{c}", [P, CHUNK], U32)
+                z_scales = tile(f"z_scales{c}", [P, CHUNK], U8)
+                quantise(nc, z_codes[:], z_scales[:], z_grouped[c][:])
+                yb_banks.append(products(wb_of, z_codes[:], z_scales[:]))
+            c = step - 1
+            if 0 <= c < CHUNKS:
+                cols = slice(c * CHUNK, (c + 1) * CHUNK)
+                for u, bank in enumerate(yb_banks[c]):
+                    pair = slice(2 * u, 2 * u + 2)
+                    nc.vector.tensor_tensor(y[c][:, pair, :], bank[:], ya[c][:, pair, :], MAX)
+                nc.sync.dma_start(out_rows[:, :, cols], y[c][:])
+                interleave(nc, y_grouped[c][:], y[c][:])
+            c = step - 2
+            if 0 <= c < CHUNKS:
+                cols = slice(c * CHUNK, (c + 1) * CHUNK)
+                quantise(nc, y_codes[:, cols], y_scales[:, cols], y_grouped[c][:])
+                nc.sync.dma_start(out_words[:, cols], y_codes[:, cols].bitcast(I32))
+        for q in range(4):
+            queue = nc.sync if q % 2 == 0 else nc.scalar
+            queue.dma_start(
+                out_2[0, 4 * q : 4 * q + 4, :].bitcast(I32), y_scales[32 * q : 32 * q + 4, :].bitcast(I32)
+            )

@@ -1,6 +1,7 @@
 from contextlib import ExitStack
 
 import concourse.mybir as mybir
+from concourse.masks import make_identity
 
 K, L, N, T, J = 512, 512, 512, 2048, 1024
 FLOPS = 2 * (K + L) * N * J
@@ -20,12 +21,16 @@ P = 128
 PACK = 4
 GROUP = 16
 X_PIECE = 512
-CHUNK = 256
-CHUNKS = J // CHUNK
+HALF = J // 2
+PIECE = 256
+WIDTHS = (128, 256, 256, 256, 128)
+STARTS = tuple(sum(WIDTHS[:c]) for c in range(len(WIDTHS)))
+CHUNKS = len(WIDTHS)
+BANK = 512
 
 
-def interleave(nc, out, planes):
-    nc.scalar.copy(
+def interleave(copy, out, planes):
+    copy(
         out=out.rearrange("p (c e) i -> p c i e", e=4),
         in_=planes.rearrange("p i (c e) -> p c i e", e=4),
     )
@@ -41,16 +46,16 @@ def tile_list_max_noneP_kernel(
     nc = tc.nc
     with ExitStack() as ctx:
         sb = ctx.enter_context(tc.tile_pool(name="sb", bufs=1))
-        psum = ctx.enter_context(tc.psum_pool(name="psum", bufs=4))
+        psum = ctx.enter_context(tc.psum_pool(name="psum", bufs=8))
 
-        def tile(name, shape, dtype):
-            return sb.tile(shape, dtype, name=name, align_bytes=64)
+        def tile(name, shape, dtype, tag=None):
+            return sb.tile(shape, dtype, name=name, tag=tag or name, align_bytes=64)
 
         x_list = sb.tile([P, J // GROUP], U16, name="x_list")
         z_list = sb.tile([P, J // GROUP], U16, name="z_list")
         x_planes = [tile(f"x_plane{i}", [P, T], F32) for i in range(PACK)]
         z_planes = [tile(f"z_plane{i}", [P, T], F32) for i in range(PACK)]
-        x_wgt = [tile(f"x_wgt{h}", [P, X_PIECE], F32) for h in range(J // X_PIECE)]
+        x_wgt = tile("x_wgt", [P, J], F32)
         z_wgt = tile("z_wgt", [P, J], F32)
         wa_raw = tile("wa_raw", [P, 2 * N], U8)
         wa_scales_raw = tile("wa_scales_raw", [P, N], U8)
@@ -60,6 +65,10 @@ def tile_list_max_noneP_kernel(
         z_rows = zT.rearrange("(p i) t -> p i t", i=PACK)
 
         nc.vector.memset(wa_scales_raw[:].bitcast(I32), 0)
+        head_rows = tile("head_rows", [P, HALF], F32)
+        nc.gpsimd.memset(head_rows[:], 0.0)
+        identity = tile("identity", [P, P], F32)
+        make_identity(nc, identity[:])
         nc.sync.dma_start(x_list[:], offs)
         nc.sync.dma_start(x_planes[0][:], x_rows[:, 0, :])
         nc.scalar.dma_start(wa_raw[:].bitcast(I32), wa_words[0].bitcast(I32))
@@ -67,14 +76,17 @@ def tile_list_max_noneP_kernel(
             nc.scalar.dma_start(
                 wa_scales_raw[32 * q : 32 * q + 4, :].bitcast(I32), wa_scales[0, 4 * q : 4 * q + 4, :].bitcast(I32)
             )
-        for h in range(J // X_PIECE):
-            nc.sync.dma_start(x_wgt[h][:], wgt[:, h * X_PIECE : (h + 1) * X_PIECE])
-        for i in range(1, PACK):
+        nc.sync.dma_start(x_wgt[:, :PIECE], wgt[:, :PIECE])
+        nc.sync.dma_start(x_wgt[:, PIECE:], wgt[:, PIECE:])
+        nc.sync.dma_start(x_planes[1][:], x_rows[:, 1, :])
+        half_rows = wgt2.rearrange("p (h j) -> (p h) j", h=2)
+        nc.sync.dma_start(head_rows[0:P:8, :], half_rows[0 : 2 * P : GROUP + 1, :])
+        for i in range(2, PACK):
             nc.sync.dma_start(x_planes[i][:], x_rows[:, i, :])
-        nc.sync.dma_start(wb_raw[:], wb.rearrange("(p i) n -> p i n", i=PACK))
         nc.sync.dma_start(z_list[:], offs2)
-        nc.sync.dma_start(z_wgt[:], wgt2)
-        for i in range(PACK):
+        nc.sync.dma_start(z_planes[0][:], z_rows[:, 0, :])
+        nc.sync.dma_start(wb_raw[:], wb.rearrange("(p i) n -> p i n", i=PACK))
+        for i in range(1, PACK):
             nc.sync.dma_start(z_planes[i][:], z_rows[:, i, :])
 
         wa_codes = tile("wa_codes", [P, 2 * N], U8)
@@ -88,92 +100,163 @@ def tile_list_max_noneP_kernel(
             in_=wa_scales_raw[:].rearrange("p (m t) -> p m t", t=PACK),
         )
 
-        def gather(picked, planes, i, offsets, j0, width, weights):
+        blocks = HALF // P
+        turned = psum.tile([P, blocks, P], F32, name="bank")
+        for v in range(blocks):
+            nc.tensor.transpose(turned[:, v, :], head_rows[:, v * P : (v + 1) * P], identity[:])
+        for h in range(2):
+            spread = tile(f"spread{h}", [P, blocks, P], F32)
+            nc.scalar.copy(
+                out=spread[:].rearrange("j v (g r) -> j v g r", r=GROUP),
+                in_=turned[:].rearrange("j v (g r) -> j v g r", r=GROUP)[:, :, :, 8 * h : 8 * h + 1].to_broadcast(
+                    [P, blocks, P // GROUP, GROUP]
+                ),
+            )
+            back = psum.tile([P, blocks, P], F32, name="bank")
+            for v in range(blocks):
+                nc.tensor.transpose(back[:, v, :], spread[:, v, :], identity[:])
+            nc.scalar.copy(out=z_wgt[:, h * HALF : (h + 1) * HALF], in_=back[:].rearrange("p v j -> p (v j)"))
+
+        def gather(picked, planes, i, offsets, weights, j0, j1):
             nc.vector.tensor_tensor(
-                picked[:, i, :], planes[i][:].indirect(offsets[:, j0 // GROUP : (j0 + width) // GROUP]), weights, MULT
+                picked[:, i * J + j0 : i * J + j1],
+                planes[i][:].indirect(offsets[:, j0 // GROUP : j1 // GROUP]),
+                weights[:, j0:j1],
+                MULT,
             )
 
-        def products(lhs_of, codes, scales):
+        def columns(picked, j0, j1):
+            return picked[:].rearrange("p (i j) -> p i j", i=PACK)[:, :, j0:j1]
+
+        def products(lhs_of, codes, scales, width):
+            slices = BANK // width
             banks = []
-            for u in range(2):
-                bank = psum.tile([P, 2, CHUNK], F32, name="bank", bufs=8)
-                for v in range(2):
-                    lhs, lhs_scale = lhs_of(2 * u + v)
+            for t0 in range(0, PACK, slices):
+                bank = psum.tile([P, slices, width], F32, name="bank")
+                for v in range(slices):
+                    lhs, lhs_scale = lhs_of(t0 + v)
                     nc.tensor.matmul_mx(
                         out=bank[:, v, :], lhsT=lhs, lhsT_scale=lhs_scale,
                         rhs=codes.bitcast(FP8X4), rhs_scale=scales, start=True, stop=True,
                     )
-                banks.append(bank)
+                banks.append((slice(t0, t0 + slices), bank))
             return banks
 
         def wa_of(t):
             return wa_codes[:, 2 * P * t : 2 * P * (t + 1)].bitcast(FP4X4), wa_plane[:, P * t : P * (t + 1)]
 
-        x_picked = [tile(f"x_picked{h}", [P, PACK, X_PIECE], F32) for h in range(J // X_PIECE)]
-        for i in range(PACK):
-            for h in range(J // X_PIECE):
-                gather(x_picked[h], x_planes, i, x_list, h * X_PIECE, X_PIECE, x_wgt[h][:])
-        ya = [tile(f"ya{c}", [P, PACK, CHUNK], F32) for c in range(CHUNKS)]
-        x_grouped = [tile(f"x_grouped{h}", [P, X_PIECE, PACK], BF16) for h in range(J // X_PIECE)]
-        for h in range(J // X_PIECE):
-            interleave(nc, x_grouped[h][:], x_picked[h][:])
+        x_picked = tile("x_picked", [P, PACK * J], F32)
+        x_cuts = [(0, PIECE, J), (0, J), (0, J), (0, X_PIECE // 2, X_PIECE, J)]
+        def gather_x(i):
+            for j0, j1 in zip(x_cuts[i], x_cuts[i][1:]):
+                gather(x_picked, x_planes, i, x_list, x_wgt, j0, j1)
+
+        gather_x(0)
+        gather_x(1)
+        gather_x(2)
+        gather_x(3)
+        x_grouped = [tile(f"x_grouped{h}", [P, X_PIECE, PACK], BF16, tag=f"spread{1 - h}") for h in range(J // X_PIECE)]
+        for j0, j1 in zip(x_cuts[3], x_cuts[3][1:]):
+            h = j0 // X_PIECE
+            interleave(nc.scalar.copy, x_grouped[h][:, j0 - h * X_PIECE : j1 - h * X_PIECE, :], columns(x_picked, j0, j1))
+
         wb_grouped = tile("wb_grouped", [P, N, PACK], BF16)
         nc.scalar.copy(
             out=wb_grouped[:].rearrange("p (t m) i -> p m i t", t=PACK),
             in_=wb_raw[:].rearrange("p i (m t) -> p m i t", t=PACK),
         )
-        for h in range(J // X_PIECE):
-            x_codes = tile(f"x_codes{h}", [P, X_PIECE], U32)
-            x_scales = tile(f"x_scales{h}", [P, X_PIECE], U8)
-            quantise(nc, x_codes[:], x_scales[:], x_grouped[h][:])
-            for s in range(X_PIECE // CHUNK):
-                cols = slice(s * CHUNK, (s + 1) * CHUNK)
-                c = h * (X_PIECE // CHUNK) + s
-                for u, bank in enumerate(products(wa_of, x_codes[:, cols], x_scales[:, cols])):
-                    nc.scalar.copy(out=ya[c][:, 2 * u : 2 * u + 2, :], in_=bank[:])
 
-        wb_codes = tile("wb_codes", [P, N], U32)
+        z_picked = tile("z_picked", [P, PACK * J], F32)
+        gather(z_picked, z_planes, 0, z_list, z_wgt, 0, J)
+
+        x_codes = tile("x_codes", [P, J], U32, tag="z_plane0")
+        x_scales = tile("x_scales", [P, J], U8)
+        quantise(nc, x_codes[:, :X_PIECE], x_scales[:, :X_PIECE], x_grouped[0][:])
+        quantise(nc, x_codes[:, X_PIECE:], x_scales[:, X_PIECE:], x_grouped[1][:])
+        ya = [tile(f"ya{c}", [P, PACK, WIDTHS[c]], F32, tag="wb_raw" if c == 0 else None) for c in range(CHUNKS)]
+        for c in range(CHUNKS):
+            cols = slice(STARTS[c], STARTS[c] + WIDTHS[c])
+            for rows, bank in products(wa_of, x_codes[:, cols], x_scales[:, cols], WIDTHS[c]):
+                nc.scalar.copy(out=ya[c][:, rows, :], in_=bank[:])
+
+        gather(z_picked, z_planes, 1, z_list, z_wgt, 0, J)
+        gather(z_picked, z_planes, 2, z_list, z_wgt, 0, J)
+        wb_codes = tile("wb_codes", [P, N], U32, tag="z_plane2")
         wb_plane = tile("wb_plane", [P, N], U8)
         quantise(nc, wb_codes[:], wb_plane[:], wb_grouped[:])
 
         def wb_of(t):
             return wb_codes[:, P * t : P * (t + 1)].bitcast(FP8X4), wb_plane[:, P * t : P * (t + 1)]
 
-        z_picked = [tile(f"z_picked{c}", [P, PACK, CHUNK], F32) for c in range(CHUNKS)]
-        for i in range(PACK):
-            for c in range(CHUNKS):
-                gather(z_picked[c], z_planes, i, z_list, c * CHUNK, CHUNK, z_wgt[:, c * CHUNK : (c + 1) * CHUNK])
-        z_grouped = [tile(f"z_grouped{c}", [P, CHUNK, PACK], BF16) for c in range(CHUNKS)]
-        for c in range(CHUNKS):
-            interleave(nc, z_grouped[c][:], z_picked[c][:])
-
+        held = (PACK - 1) * J + STARTS[2]
+        z_grouped = [z_picked[:, held : held + 2 * WIDTHS[0]].bitcast(BF16).rearrange("p (j i) -> p j i", i=PACK)]
+        z_grouped = z_grouped + [tile(f"z_grouped{c}", [P, WIDTHS[c], PACK], BF16)[:] for c in range(1, CHUNKS)]
         y_codes = tile("y_codes", [P, J], U32)
         y_scales = tile("y_scales", [P, J], U8)
         out_rows = out_0.rearrange("(p t) j -> p t j", t=PACK)
         out_words = out_1[0].rearrange("p j i -> p (j i)").bitcast(I32)
-        y = [tile(f"y{c}", [P, PACK, CHUNK], F32) for c in range(CHUNKS)]
-        y_grouped = [tile(f"y_grouped{c}", [P, CHUNK, PACK], BF16) for c in range(CHUNKS)]
-        yb_banks = []
-        for step in range(CHUNKS + 2):
-            c = step
-            if c < CHUNKS:
-                z_codes = tile(f"z_codes{c}", [P, CHUNK], U32)
-                z_scales = tile(f"z_scales{c}", [P, CHUNK], U8)
-                quantise(nc, z_codes[:], z_scales[:], z_grouped[c][:])
-                yb_banks.append(products(wb_of, z_codes[:], z_scales[:]))
-            c = step - 1
-            if 0 <= c < CHUNKS:
-                cols = slice(c * CHUNK, (c + 1) * CHUNK)
-                for u, bank in enumerate(yb_banks[c]):
-                    pair = slice(2 * u, 2 * u + 2)
-                    nc.vector.tensor_tensor(y[c][:, pair, :], bank[:], ya[c][:, pair, :], MAX)
-                nc.sync.dma_start(out_rows[:, :, cols], y[c][:])
-                interleave(nc, y_grouped[c][:], y[c][:])
-            c = step - 2
-            if 0 <= c < CHUNKS:
-                cols = slice(c * CHUNK, (c + 1) * CHUNK)
-                quantise(nc, y_codes[:, cols], y_scales[:, cols], y_grouped[c][:])
-                nc.sync.dma_start(out_words[:, cols], y_codes[:, cols].bitcast(I32))
+        y = [tile(f"y{c}", [P, PACK, WIDTHS[c]], F32) for c in range(CHUNKS)]
+        y_grouped = [tile(f"y_grouped{c}", [P, WIDTHS[c], PACK], BF16) for c in range(CHUNKS)]
+        yb_banks = {}
+
+        def cols_of(c):
+            return slice(STARTS[c], STARTS[c] + WIDTHS[c])
+
+        def gather_last(c):
+            gather(z_picked, z_planes, PACK - 1, z_list, z_wgt, STARTS[c], STARTS[c] + WIDTHS[c])
+
+        def interleave_z(c):
+            interleave(nc.scalar.copy, z_grouped[c], columns(z_picked, STARTS[c], STARTS[c] + WIDTHS[c]))
+
+        def multiply(c):
+            z_codes = tile(f"z_codes{c}", [P, WIDTHS[c]], U32)
+            z_scales = tile(f"z_scales{c}", [P, WIDTHS[c]], U8)
+            quantise(nc, z_codes[:], z_scales[:], z_grouped[c])
+            yb_banks.setdefault(c, products(wb_of, z_codes[:], z_scales[:], WIDTHS[c]))
+
+        def join(c):
+            for rows, bank in yb_banks[c]:
+                nc.vector.tensor_tensor(y[c][:, rows, :], bank[:], ya[c][:, rows, :], MAX)
+            nc.sync.dma_start(out_rows[:, :, cols_of(c)], y[c][:])
+
+        def round_y(c, copy):
+            interleave(copy, y_grouped[c][:], y[c][:])
+
+        def store_codes(j0, j1):
+            nc.sync.dma_start(out_words[:, j0:j1], y_codes[:, j0:j1].bitcast(I32))
+
+        def hand_on(c):
+            quantise(nc, y_codes[:, cols_of(c)], y_scales[:, cols_of(c)], y_grouped[c][:])
+
+        gather_last(0)
+        gather_last(1)
+        interleave_z(0)
+        multiply(0)
+        gather_last(2)
+        gather(z_picked, z_planes, PACK - 1, z_list, z_wgt, STARTS[3], J)
+        for c in range(1, CHUNKS):
+            interleave_z(c)
+        multiply(1)
+        join(0)
+        round_y(0, nc.scalar.copy)
+        multiply(2)
+        join(1)
+        round_y(1, nc.scalar.copy)
+        multiply(3)
+        multiply(4)
+        join(2)
+        round_y(2, nc.scalar.copy)
+        join(3)
+        round_y(3, nc.scalar.copy)
+        hand_on(0)
+        hand_on(1)
+        join(4)
+        hand_on(2)
+        store_codes(0, STARTS[3])
+        round_y(4, nc.vector.tensor_copy)
+        hand_on(3)
+        hand_on(4)
+        store_codes(STARTS[3], J)
         for q in range(4):
             queue = nc.sync if q % 2 == 0 else nc.scalar
             queue.dma_start(

@@ -90,14 +90,9 @@ def tile_list_max_noneP_kernel(
             nc.sync.dma_start(z_planes[i][:], z_rows[:, i, :])
 
         wa_codes = tile("wa_codes", [P, 2 * N], U8)
-        wa_plane = tile("wa_plane", [P, N], U8)
         nc.vector.tensor_copy(
             out=wa_codes[:].rearrange("p (t m b) -> p m t b", t=PACK, b=2),
             in_=wa_raw[:].rearrange("p (m t b) -> p m t b", t=PACK, b=2),
-        )
-        nc.vector.tensor_copy(
-            out=wa_plane[:].rearrange("p (t m) -> p m t", t=PACK),
-            in_=wa_scales_raw[:].rearrange("p (m t) -> p m t", t=PACK),
         )
 
         blocks = HALF // P
@@ -152,6 +147,11 @@ def tile_list_max_noneP_kernel(
                 gather(x_picked, x_planes, i, x_list, x_wgt, j0, j1)
 
         gather_x(0)
+        wa_plane = tile("wa_plane", [P, N], U8, tag="x_plane0")
+        nc.vector.tensor_copy(
+            out=wa_plane[:].rearrange("p (t m) -> p m t", t=PACK),
+            in_=wa_scales_raw[:].rearrange("p (m t) -> p m t", t=PACK),
+        )
         gather_x(1)
         gather_x(2)
         gather_x(3)

from contextlib import ExitStack

import concourse.mybir as mybir
from concourse.masks import make_identity

K, L, N, T, J = 512, 512, 512, 2048, 1024
FLOPS = 2 * (K + L) * N * J

F32 = mybir.dt.float32
BF16 = mybir.dt.bfloat16
I32 = mybir.dt.int32
U32 = mybir.dt.uint32
U16 = mybir.dt.uint16
U8 = mybir.dt.uint8
FP8X4 = mybir.dt.float8_e4m3fn_x4
FP4X4 = mybir.dt.float4_e2m1fn_x4
MULT = mybir.AluOpType.mult
MAX = mybir.AluOpType.max

P = 128
PACK = 4
GROUP = 16
X_PIECE = 512
HALF = J // 2
PIECE = 256
WIDTHS = (128, 256, 256, 256, 128)
STARTS = tuple(sum(WIDTHS[:c]) for c in range(len(WIDTHS)))
CHUNKS = len(WIDTHS)
BANK = 512


def interleave(copy, out, planes):
    copy(
        out=out.rearrange("p (c e) i -> p c i e", e=4),
        in_=planes.rearrange("p i (c e) -> p c i e", e=4),
    )


def quantise(nc, codes, scales, grouped):
    nc.vector.quantize_mx(out=codes.bitcast(FP8X4), scales=scales, in_=grouped.rearrange("p j i -> p (j i)"))


def tile_list_max_noneP_kernel(
    tc, xT, wgt, zT, wgt2, wa_words, wa_scales, wb, offs, offs2, out_0, out_1, out_2
):
    nc = tc.nc
    with ExitStack() as ctx:
        sb = ctx.enter_context(tc.tile_pool(name="sb", bufs=1))
        psum = ctx.enter_context(tc.psum_pool(name="psum", bufs=8))

        def tile(name, shape, dtype, tag=None):
            return sb.tile(shape, dtype, name=name, tag=tag or name, align_bytes=64)

        x_list = sb.tile([P, J // GROUP], U16, name="x_list")
        z_list = sb.tile([P, J // GROUP], U16, name="z_list")
        x_planes = [tile(f"x_plane{i}", [P, T], F32) for i in range(PACK)]
        z_planes = [tile(f"z_plane{i}", [P, T], F32) for i in range(PACK)]
        x_wgt = tile("x_wgt", [P, J], F32)
        z_wgt = tile("z_wgt", [P, J], F32)
        wa_raw = tile("wa_raw", [P, 2 * N], U8)
        wa_scales_raw = tile("wa_scales_raw", [P, N], U8)
        wb_raw = tile("wb_raw", [P, PACK, N], F32)

        x_rows = xT.rearrange("(p i) t -> p i t", i=PACK)
        z_rows = zT.rearrange("(p i) t -> p i t", i=PACK)

        nc.vector.memset(wa_scales_raw[:].bitcast(I32), 0)
        head_rows = tile("head_rows", [P, HALF], F32)
        nc.gpsimd.memset(head_rows[:], 0.0)
        identity = tile("identity", [P, P], F32)
        make_identity(nc, identity[:])
        nc.sync.dma_start(x_list[:], offs)
        nc.sync.dma_start(x_planes[0][:], x_rows[:, 0, :])
        nc.scalar.dma_start(wa_raw[:].bitcast(I32), wa_words[0].bitcast(I32))
        for q in range(4):
            nc.scalar.dma_start(
                wa_scales_raw[32 * q : 32 * q + 4, :].bitcast(I32), wa_scales[0, 4 * q : 4 * q + 4, :].bitcast(I32)
            )
        nc.sync.dma_start(x_wgt[:, :PIECE], wgt[:, :PIECE])
        nc.sync.dma_start(x_wgt[:, PIECE:], wgt[:, PIECE:])
        nc.sync.dma_start(x_planes[1][:], x_rows[:, 1, :])
        half_rows = wgt2.rearrange("p (h j) -> (p h) j", h=2)
        nc.sync.dma_start(head_rows[0:P:8, :], half_rows[0 : 2 * P : GROUP + 1, :])
        for i in range(2, PACK):
            nc.sync.dma_start(x_planes[i][:], x_rows[:, i, :])
        nc.sync.dma_start(z_list[:], offs2)
        nc.sync.dma_start(z_planes[0][:], z_rows[:, 0, :])
        nc.sync.dma_start(wb_raw[:], wb.rearrange("(p i) n -> p i n", i=PACK))
        for i in range(1, PACK):
            nc.sync.dma_start(z_planes[i][:], z_rows[:, i, :])

        wa_codes = tile("wa_codes", [P, 2 * N], U8)
        nc.vector.tensor_copy(
            out=wa_codes[:].rearrange("p (t m b) -> p m t b", t=PACK, b=2),
            in_=wa_raw[:].rearrange("p (m t b) -> p m t b", t=PACK, b=2),
        )

        blocks = HALF // P
        turned = psum.tile([P, blocks, P], F32, name="bank")
        for v in range(blocks):
            nc.tensor.transpose(turned[:, v, :], head_rows[:, v * P : (v + 1) * P], identity[:])
        for h in range(2):
            spread = tile(f"spread{h}", [P, blocks, P], F32)
            nc.scalar.copy(
                out=spread[:].rearrange("j v (g r) -> j v g r", r=GROUP),
                in_=turned[:].rearrange("j v (g r) -> j v g r", r=GROUP)[:, :, :, 8 * h : 8 * h + 1].to_broadcast(
                    [P, blocks, P // GROUP, GROUP]
                ),
            )
            back = psum.tile([P, blocks, P], F32, name="bank")
            for v in range(blocks):
                nc.tensor.transpose(back[:, v, :], spread[:, v, :], identity[:])
            nc.scalar.copy(out=z_wgt[:, h * HALF : (h + 1) * HALF], in_=back[:].rearrange("p v j -> p (v j)"))

        def gather(picked, planes, i, offsets, weights, j0, j1):
            nc.vector.tensor_tensor(
                picked[:, i * J + j0 : i * J + j1],
                planes[i][:].indirect(offsets[:, j0 // GROUP : j1 // GROUP]),
                weights[:, j0:j1],
                MULT,
            )

        def columns(picked, j0, j1):
            return picked[:].rearrange("p (i j) -> p i j", i=PACK)[:, :, j0:j1]

        def products(lhs_of, codes, scales, width):
            slices = BANK // width
            banks = []
            for t0 in range(0, PACK, slices):
                bank = psum.tile([P, slices, width], F32, name="bank")
                for v in range(slices):
                    lhs, lhs_scale = lhs_of(t0 + v)
                    nc.tensor.matmul_mx(
                        out=bank[:, v, :], lhsT=lhs, lhsT_scale=lhs_scale,
                        rhs=codes.bitcast(FP8X4), rhs_scale=scales, start=True, stop=True,
                    )
                banks.append((slice(t0, t0 + slices), bank))
            return banks

        def wa_of(t):
            return wa_codes[:, 2 * P * t : 2 * P * (t + 1)].bitcast(FP4X4), wa_plane[:, P * t : P * (t + 1)]

        x_picked = tile("x_picked", [P, PACK * J], F32)
        x_cuts = [(0, PIECE, J), (0, J), (0, J), (0, X_PIECE // 2, X_PIECE, J)]
        def gather_x(i):
            for j0, j1 in zip(x_cuts[i], x_cuts[i][1:]):
                gather(x_picked, x_planes, i, x_list, x_wgt, j0, j1)

        gather_x(0)
        wa_plane = tile("wa_plane", [P, N], U8, tag="x_plane0")
        nc.vector.tensor_copy(
            out=wa_plane[:].rearrange("p (t m) -> p m t", t=PACK),
            in_=wa_scales_raw[:].rearrange("p (m t) -> p m t", t=PACK),
        )
        gather_x(1)
        gather_x(2)
        gather_x(3)
        x_grouped = [tile(f"x_grouped{h}", [P, X_PIECE, PACK], BF16, tag=f"spread{1 - h}") for h in range(J // X_PIECE)]
        for j0, j1 in zip(x_cuts[3], x_cuts[3][1:]):
            h = j0 // X_PIECE
            interleave(nc.scalar.copy, x_grouped[h][:, j0 - h * X_PIECE : j1 - h * X_PIECE, :], columns(x_picked, j0, j1))

        wb_grouped = tile("wb_grouped", [P, N, PACK], BF16)
        nc.scalar.copy(
            out=wb_grouped[:].rearrange("p (t m) i -> p m i t", t=PACK),
            in_=wb_raw[:].rearrange("p i (m t) -> p m i t", t=PACK),
        )

        z_picked = tile("z_picked", [P, PACK * J], F32)
        gather(z_picked, z_planes, 0, z_list, z_wgt, 0, J)

        x_codes = tile("x_codes", [P, J], U32, tag="z_plane0")
        x_scales = tile("x_scales", [P, J], U8)
        quantise(nc, x_codes[:, :X_PIECE], x_scales[:, :X_PIECE], x_grouped[0][:])
        quantise(nc, x_codes[:, X_PIECE:], x_scales[:, X_PIECE:], x_grouped[1][:])
        ya = [tile(f"ya{c}", [P, PACK, WIDTHS[c]], F32, tag="wb_raw" if c == 0 else None) for c in range(CHUNKS)]
        for c in range(CHUNKS):
            cols = slice(STARTS[c], STARTS[c] + WIDTHS[c])
            for rows, bank in products(wa_of, x_codes[:, cols], x_scales[:, cols], WIDTHS[c]):
                nc.scalar.copy(out=ya[c][:, rows, :], in_=bank[:])

        gather(z_picked, z_planes, 1, z_list, z_wgt, 0, J)
        gather(z_picked, z_planes, 2, z_list, z_wgt, 0, J)
        wb_codes = tile("wb_codes", [P, N], U32, tag="z_plane2")
        wb_plane = tile("wb_plane", [P, N], U8)
        quantise(nc, wb_codes[:], wb_plane[:], wb_grouped[:])

        def wb_of(t):
            return wb_codes[:, P * t : P * (t + 1)].bitcast(FP8X4), wb_plane[:, P * t : P * (t + 1)]

        held = (PACK - 1) * J + STARTS[2]
        z_grouped = [z_picked[:, held : held + 2 * WIDTHS[0]].bitcast(BF16).rearrange("p (j i) -> p j i", i=PACK)]
        z_grouped = z_grouped + [tile(f"z_grouped{c}", [P, WIDTHS[c], PACK], BF16)[:] for c in range(1, CHUNKS)]
        y_codes = tile("y_codes", [P, J], U32)
        y_scales = tile("y_scales", [P, J], U8)
        out_rows = out_0.rearrange("(p t) j -> p t j", t=PACK)
        out_words = out_1[0].rearrange("p j i -> p (j i)").bitcast(I32)
        y = [tile(f"y{c}", [P, PACK, WIDTHS[c]], F32) for c in range(CHUNKS)]
        y_grouped = [tile(f"y_grouped{c}", [P, WIDTHS[c], PACK], BF16) for c in range(CHUNKS)]
        yb_banks = {}

        def cols_of(c):
            return slice(STARTS[c], STARTS[c] + WIDTHS[c])

        def gather_last(c):
            gather(z_picked, z_planes, PACK - 1, z_list, z_wgt, STARTS[c], STARTS[c] + WIDTHS[c])

        def interleave_z(c):
            interleave(nc.scalar.copy, z_grouped[c], columns(z_picked, STARTS[c], STARTS[c] + WIDTHS[c]))

        def multiply(c):
            z_codes = tile(f"z_codes{c}", [P, WIDTHS[c]], U32)
            z_scales = tile(f"z_scales{c}", [P, WIDTHS[c]], U8)
            quantise(nc, z_codes[:], z_scales[:], z_grouped[c])
            yb_banks.setdefault(c, products(wb_of, z_codes[:], z_scales[:], WIDTHS[c]))

        def join(c):
            for rows, bank in yb_banks[c]:
                nc.vector.tensor_tensor(y[c][:, rows, :], bank[:], ya[c][:, rows, :], MAX)
            nc.sync.dma_start(out_rows[:, :, cols_of(c)], y[c][:])

        def round_y(c, copy):
            interleave(copy, y_grouped[c][:], y[c][:])

        def store_codes(j0, j1):
            nc.sync.dma_start(out_words[:, j0:j1], y_codes[:, j0:j1].bitcast(I32))

        def hand_on(c):
            quantise(nc, y_codes[:, cols_of(c)], y_scales[:, cols_of(c)], y_grouped[c][:])

        gather_last(0)
        gather_last(1)
        interleave_z(0)
        multiply(0)
        gather_last(2)
        gather(z_picked, z_planes, PACK - 1, z_list, z_wgt, STARTS[3], J)
        for c in range(1, CHUNKS):
            interleave_z(c)
        multiply(1)
        join(0)
        round_y(0, nc.scalar.copy)
        multiply(2)
        join(1)
        round_y(1, nc.scalar.copy)
        multiply(3)
        multiply(4)
        join(2)
        round_y(2, nc.scalar.copy)
        join(3)
        round_y(3, nc.scalar.copy)
        hand_on(0)
        hand_on(1)
        join(4)
        hand_on(2)
        store_codes(0, STARTS[3])
        round_y(4, nc.vector.tensor_copy)
        hand_on(3)
        hand_on(4)
        store_codes(STARTS[3], J)
        for q in range(4):
            queue = nc.sync if q % 2 == 0 else nc.scalar
            queue.dma_start(
                out_2[0, 4 * q : 4 * q + 4, :].bitcast(I32), y_scales[32 * q : 32 * q + 4, :].bitcast(I32)
            )
